import numpy as np
import ml_dtypes


def mxq(x, axis, fmt="e4m3"):
    dtype, down = {"e4m3": (ml_dtypes.float8_e4m3fn, 7), "e5m2": (ml_dtypes.float8_e5m2, 14)}[fmt]
    v = np.moveaxis(np.asarray(x, np.float32).astype(ml_dtypes.bfloat16).astype(np.float64), axis, -1)
    blocks = v.reshape(v.shape[:-1] + (-1, 32))
    amax = np.abs(blocks).max(-1, keepdims=True)
    byte = np.maximum(np.where(amax > 0, np.frexp(amax)[1] - 1 + 127, 0) - down, 1)
    scale = np.exp2(byte - 127.0)
    codes = (blocks / scale).astype(np.float32).astype(dtype).astype(np.float64)
    return np.moveaxis((codes * scale).reshape(v.shape), -1, axis)


WIDE = False


def mx_kscale(k):
    if not WIDE:
        return np.ones(k)
    levels = np.array([10, -10, 5, -5, 0])
    if k % 512:
        return np.exp2(np.random.permutation(np.resize(levels, k // 32))).repeat(32)
    a = np.empty((k // 512, 16))
    for p in range(k // 512):
        a[p, :8] = np.random.permutation(np.resize(levels, 8))
        for g in range(8):
            far = levels[np.abs(levels - a[p, g]) >= 10]
            a[p, g + 8] = far[np.random.randint(len(far))]
    return np.exp2(a.ravel()).repeat(32)


def f64(x):
    return np.asarray(x).astype(np.float64)


def striped(idx):
    return np.tile(np.asarray(idx).reshape(-1, 16).T, (8, 1)).astype(np.uint16)


def unstriped(offs):
    return offs[:16].T.reshape(-1).astype(np.int64)


def striped8(idx):
    return np.asarray(idx).reshape(8, -1, 16).transpose(0, 2, 1).reshape(128, -1).astype(np.uint16)


def unstriped8(offs):
    return offs.reshape(8, 16, -1).transpose(0, 2, 1).reshape(8, -1).astype(np.int64)


def pick8(x, idx, run):
    r = np.arange(len(x))
    return x[r[:, None], idx[r % (8 * run) // run]]


E2M1 = np.array([0.0, 0.5, 1.0, 1.5, 2.0, 3.0, 4.0, 6.0, -0.0, -0.5, -1.0, -1.5, -2.0, -3.0, -4.0, -6.0])


def pack_weight(w, fmt):
    k, n = w.shape
    w = f64(np.asarray(w, np.float32).astype(ml_dtypes.bfloat16)).reshape(k // 32, 32, n)
    amax = np.abs(w).max(1)
    if fmt == "e4m3":
        byte = np.frexp(amax)[1] - 1 + 127 - 7
    else:
        mant, ex = np.frexp(amax / 6.0)
        byte = np.where(mant > 0.5, ex, ex - 1) + 127
    byte = np.clip(np.where(amax > 0, byte, 1), 1, 254)
    scaled = (w * np.exp2(127.0 - byte)[:, None, :]).reshape(k, n).astype(np.float32)
    by_word = np.ascontiguousarray(scaled.reshape(k // 512, 128, 4, n).transpose(0, 1, 3, 2))
    if fmt == "e4m3":
        words = by_word.astype(ml_dtypes.float8_e4m3fn).view(np.uint8)
    else:
        c = by_word.astype(ml_dtypes.float4_e2m1fn).view(np.uint8) & 0xF
        words = (c[..., 0::2] | (c[..., 1::2] << 4)).reshape(k // 512, 128, 2 * n)
    return np.ascontiguousarray(words), np.ascontiguousarray(byte.astype(np.uint8).reshape(k // 512, 16, n))


def unpack_weight(words, scales, fmt):
    g, _, n = scales.shape
    words = np.ascontiguousarray(words).reshape(g, 128, n, -1)
    if fmt == "e4m3":
        vals = words.view(ml_dtypes.float8_e4m3fn).astype(np.float64)
    else:
        nib = np.empty((g, 128, n, 4), np.uint8)
        nib[..., 0::2] = words & 0xF
        nib[..., 1::2] = words >> 4
        vals = E2M1[nib]
    vals = vals * np.repeat(np.exp2(scales.astype(np.float64) - 127.0), 8, axis=1)[..., None]
    return vals.transpose(0, 1, 3, 2).reshape(g * 512, n)


K, J, R, T, U, F, C, O, N, S, Z = 512, 256, 512, 1024, 512, 1024, 512, 128, 256, 512, 1024


def setup_inputs():
    n = np.random.standard_normal
    idx = np.stack([np.random.permutation(T)[:U] for _ in range(8)])
    idx2 = np.random.permutation(U)[:J]
    idx3 = np.stack([np.random.permutation(F)[:R] for _ in range(8)])
    idx4 = np.random.permutation(C)[:J]
    idx5 = np.random.permutation(C)[:O]
    idx6 = np.stack([np.random.permutation(C)[:O] for _ in range(8)])
    idx7 = np.random.permutation(Z)[:O]
    fk = mx_kscale(K)
    fr = mx_kscale(R)
    fs = mx_kscale(S)
    wbp = pack_weight(n((R, N)) * 1 / np.sqrt(R) / fr[:, None], "e2m1")
    xrp = pack_weight(n((S, Z)) / fs[:, None], "e2m1")
    wsp = pack_weight(n((S, N)) * 1 / np.sqrt(S) * fs[:, None], "e4m3")
    return {
        "ta": (np.random.randint(-7, 8, (K, T)).astype(np.float64)).astype(np.float32),
        "ga": ((np.random.randint(8, 25, (K, 1)) / 64.0) * fk[:, None]).astype(np.float32),
        "gb": (np.random.uniform(0.5, 1.6, (K, 1))).astype(np.float32),
        "ua": (np.random.randint(-7, 8, (K, F)).astype(np.float64)).astype(np.float32),
        "ha": ((np.random.randint(8, 25, (K, 1)) / 1024.0) / fk[:, None]).astype(np.float32),
        "sa": (np.random.uniform(0.5, 1.6, (R, 1)) * fr[:, None]).astype(np.float32),
        "sb": (np.random.uniform(0.5, 1.6, (R, 1)) * fr[:, None]).astype(np.float32),
        "wb_words": wbp[0],
        "wb_scales": wbp[1],
        "xr_words": xrp[0],
        "xr_scales": xrp[1],
        "ws_words": wsp[0],
        "ws_scales": wsp[1],
        "offs": striped8(idx),
        "offs2": striped(idx2),
        "offs3": striped8(idx3),
        "offs4": striped(idx4),
        "offs5": striped(idx5),
        "offs6": striped8(idx6),
        "offs7": striped(idx7),
    }


def reference(ta, ga, gb, ua, ha, sa, sb, wb_words, wb_scales, xr_words, xr_scales, ws_words, ws_scales, offs, offs2, offs3, offs4, offs5, offs6, offs7):
    idx = unstriped8(offs)
    idx2 = unstriped(offs2)
    idx3 = unstriped8(offs3)
    idx4 = unstriped(offs4)
    idx5 = unstriped(offs5)
    idx6 = unstriped8(offs6)
    idx7 = unstriped(offs7)
    wbu = unpack_weight(wb_words, wb_scales, "e2m1")
    xru = unpack_weight(xr_words, xr_scales, "e2m1")
    wsu = unpack_weight(ws_words, ws_scales, "e4m3")
    xcd = pick8(f64(ta), idx, 64) * f64(ga)
    xc = xcd[:, idx2] * f64(gb)
    wc = pick8(f64(ua), idx3, 64) * f64(ha)
    wcq = mxq(wc, 0, "e4m3")
    xcq = mxq(xc, 0, "e4m3")
    a = wcq.T @ xcq
    pw = np.zeros((R, C))
    pw[:, idx4] = a
    hid = np.abs(pw[:, idx5] * f64(sa) - pick8(pw, idx6, 64) * f64(sb))
    hidq = mxq(hid, 0, "e4m3")
    xridx7g = xru[:, idx7]
    y = wbu.T @ hidq + wsu.T @ xridx7g
    return y

@@ -1,0 +1,232 @@
+from contextlib import ExitStack
+
+import concourse.mybir as mybir
+
+K, J, R, T, U, F, C, O, N, S, Z = 512, 256, 512, 1024, 512, 1024, 512, 128, 256, 512, 1024
+FLOPS = 2 * (K * R * J + R * N * O + S * N * O)
+
+F32 = mybir.dt.float32
+BF16 = mybir.dt.bfloat16
+I32 = mybir.dt.int32
+U32 = mybir.dt.uint32
+U16 = mybir.dt.uint16
+U8 = mybir.dt.uint8
+FP8X4 = mybir.dt.float8_e4m3fn_x4
+FP4X4 = mybir.dt.float4_e2m1fn_x4
+ACT = mybir.ActivationFunctionType
+ALU = mybir.AluOpType
+
+P = 128
+PACK = 4
+HALVES = 2
+JH = J // HALVES
+LIST_ROWS = 16
+
+
+def tile_picked_respelled_codes_one_boardmixed_reminder_plain_kernel(
+    tc, ta, ga, gb, ua, ha, sa, sb, wb_words, wb_scales, xr_words, xr_scales, ws_words, ws_scales,
+    offs, offs2, offs3, offs4, offs5, offs6, offs7, out,
+):
+    nc = tc.nc
+    with ExitStack() as ctx:
+        keep = ctx.enter_context(tc.tile_pool(name="keep", bufs=1))
+        psum = ctx.enter_context(tc.psum_pool(name="psum", bufs=1))
+
+        def load_list(name, src):
+            tile = keep.tile([P, src.shape[1]], U16, name=name)
+            nc.sync.dma_start(tile[:], src)
+            return tile
+
+        def load_factors(name, src):
+            tile = keep.tile([P, PACK], F32, name=name)
+            nc.sync.dma_start(out=tile[:], in_=src.rearrange("(p t) one -> p (t one)", t=PACK))
+            return tile
+
+        def load_rows(name, src, t):
+            tile = keep.tile([P, src.shape[1]], F32, name=name, tag=name, align_bytes=64)
+            nc.sync.dma_start(out=tile[:], in_=src.rearrange("(p t) c -> p t c", t=PACK)[:, t, :])
+            return tile
+
+        def load_words(name, src, dtype, width):
+            tile = keep.tile([P, width], dtype, name=name, align_bytes=64)
+            nc.sync.dma_start(out=tile[:].bitcast(I32), in_=src.bitcast(I32))
+            return tile
+
+        def load_scales(name, src):
+            tile = keep.tile([P, src.shape[2]], U8, name=name, align_bytes=64)
+            nc.gpsimd.memset(tile[:].bitcast(I32), 0)
+            for q in range(4):
+                nc.gpsimd.dma_start(
+                    out=tile[32 * q : 32 * q + 4, :].bitcast(I32),
+                    in_=src[0, 4 * q : 4 * q + 4, :].bitcast(I32),
+                )
+            return tile
+
+        def fetch(dst, window, offsets, factor):
+            nc.scalar.activation(out=dst, in_=window[:].indirect(offsets), func=ACT.Copy, scale=factor)
+
+        ua_rows = [load_rows("ua0", ua, 0)]
+        l3 = load_list("l3", offs3)
+        ha_t = load_factors("ha_t", ha)
+        ua_rows.extend([load_rows("ua%d" % t, ua, t) for t in range(1, PACK)])
+        l1 = load_list("l1", offs)
+        ga_t = load_factors("ga_t", ga)
+        ta_rows = [load_rows("ta0", ta, 0)]
+        l2 = load_list("l2", offs2)
+        gb_t = load_factors("gb_t", gb)
+        ta_rows.extend([load_rows("ta%d" % t, ta, t) for t in range(1, PACK)])
+        xr_w = load_words("xr_w", xr_words[0], U16, Z)
+        l7 = load_list("l7", offs7)
+        l4 = load_list("l4", offs4)
+        ws_w = load_words("ws_w", ws_words[0].rearrange("p n t -> p (n t)"), U32, N)
+        wb_w = load_words("wb_w", wb_words[0], U16, N)
+        l5 = load_list("l5", offs5)
+        l6 = load_list("l6", offs6)
+        sa_t = load_factors("sa_t", sa)
+        sb_t = load_factors("sb_t", sb)
+        xr_s = load_scales("xr_s", xr_scales)
+        ws_s = load_scales("ws_s", ws_scales)
+        wb_s = load_scales("wb_s", wb_scales)
+
+        board = [keep.tile([P, C], F32, name="board%d" % t) for t in range(PACK)]
+        for t in range(PACK):
+            nc.vector.memset(board[t][:], 0.0)
+
+        wc_rows = keep.tile([P, PACK, R], BF16, align_bytes=64)
+        for t in range(PACK):
+            fetch(wc_rows[:, t, :], ua_rows[t], l3[:], ha_t[:, t : t + 1])
+        wc_dealt = keep.tile([P, R * PACK], BF16, align_bytes=64)
+        nc.vector.tensor_copy(
+            out=wc_dealt[:].rearrange("p (d m t) -> p d m t", d=PACK, t=PACK),
+            in_=wc_rows[:].rearrange("p t (m d) -> p d m t", d=PACK),
+        )
+        wc_codes = keep.tile([P, R], U32, align_bytes=64)
+        wc_scales = keep.tile([P, R], U8, align_bytes=64)
+        nc.vector.quantize_mx(out=wc_codes[:].bitcast(FP8X4), scales=wc_scales[:], in_=wc_dealt[:])
+
+        xcd = [keep.tile([P, U], F32, name="xcd%d" % t) for t in range(PACK)]
+        xc_rows = [keep.tile([P, PACK, JH], BF16, name="xc_rows0", align_bytes=64)]
+        cols = JH // LIST_ROWS
+
+        def fetch_xc(h, t):
+            fetch(xc_rows[h][:, t, :], xcd[t], l2[:, h * cols : (h + 1) * cols], gb_t[:, t : t + 1])
+
+        for t in range(PACK):
+            fetch(xcd[t][:], ta_rows[t], l1[:], ga_t[:, t : t + 1])
+            if t > 0:
+                fetch_xc(0, t - 1)
+        xc_rows.append(keep.tile([P, PACK, JH], BF16, name="xc_rows1", tag="ta3", align_bytes=64))
+        fetch_xc(1, 0)
+        fetch_xc(0, PACK - 1)
+        for t in range(1, PACK):
+            fetch_xc(1, t)
+
+        xr_gw = keep.tile([P, O], U16, align_bytes=64)
+        xr_gs = keep.tile([P, O], U8, align_bytes=64)
+        nc.vector.tensor_copy(out=xr_gw[:], in_=xr_w[:].indirect(l7[:]))
+        nc.vector.tensor_copy(out=xr_gs[:], in_=xr_s[:].indirect(l7[:]))
+        acc = [psum.tile([P, O], F32, name="acc%d" % b) for b in range(N // P)]
+        for b in range(N // P):
+            nc.tensor.matmul_mx(
+                out=acc[b][:],
+                lhsT=ws_w[:, b * P : (b + 1) * P].bitcast(FP8X4),
+                lhsT_scale=ws_s[:, b * P : (b + 1) * P],
+                rhs=xr_gw[:].bitcast(FP4X4),
+                rhs_scale=xr_gs[:],
+                start=True,
+                stop=False,
+            )
+
+        a_sb = []
+        a_ps = []
+        for h in range(HALVES):
+            woven = keep.tile([P, JH, PACK], BF16, name="xc_woven%d" % h, tag="xc_woven", align_bytes=64)
+            nc.vector.tensor_copy(out=woven[:], in_=xc_rows[h][:].rearrange("p t j -> p j t"))
+            codes = keep.tile([P, JH], U32, name="xc_codes%d" % h, align_bytes=64)
+            scales = keep.tile([P, JH], U8, name="xc_scales%d" % h, align_bytes=64)
+            nc.vector.quantize_mx(
+                out=codes[:].bitcast(FP8X4), scales=scales[:], in_=woven[:].rearrange("p j t -> p (j t)")
+            )
+            banks = [psum.tile([P, 2, JH], F32, name="a_ps%d_%d" % (h, u)) for u in range(2)]
+            for d in range(PACK):
+                nc.tensor.matmul_mx(
+                    out=banks[d // 2][:, d % 2, :],
+                    lhsT=wc_codes[:, d * P : (d + 1) * P].bitcast(FP8X4),
+                    lhsT_scale=wc_scales[:, d * P : (d + 1) * P],
+                    rhs=codes[:].bitcast(FP8X4),
+                    rhs_scale=scales[:],
+                    start=True,
+                    stop=True,
+                )
+            a_ps.append(banks)
+            a_sb.append([keep.tile([P, 2, JH], F32, name="a_sb%d_%d" % (h, u)) for u in range(2)])
+
+        def empty(on_scalar, h, u):
+            if on_scalar:
+                nc.scalar.copy(out=a_sb[h][u][:], in_=a_ps[h][u][:])
+            else:
+                nc.vector.tensor_copy(out=a_sb[h][u][:], in_=a_ps[h][u][:])
+
+        def put(on_scalar, h, d):
+            dst = board[d][:].indirect(l4[:, h * cols : (h + 1) * cols])
+            src = a_sb[h][d // 2][:, d % 2, :]
+            if on_scalar:
+                nc.scalar.activation(out=dst, in_=src, func=ACT.Copy)
+            else:
+                nc.vector.tensor_copy(out=dst, in_=src)
+
+        first = keep.tile([P, PACK, O], F32)
+        second = keep.tile([P, PACK, O], F32)
+        diff = keep.tile([P, PACK, O], F32)
+
+        def read_board(d):
+            fetch(first[:, d, :], board[d], l5[:], sa_t[:, d : d + 1])
+            fetch(second[:, d, :], board[d], l6[:], sb_t[:, d : d + 1])
+
+        def subtract(d):
+            nc.vector.tensor_tensor(out=diff[:, d, :], in0=first[:, d, :], in1=second[:, d, :], op=ALU.subtract)
+
+        empty(True, 0, 0)
+        empty(True, 0, 1)
+        put(True, 0, 0)
+        put(False, 0, 1)
+        put(True, 0, 3)
+        put(False, 0, 2)
+        empty(True, 1, 0)
+        empty(False, 1, 1)
+        put(True, 1, 0)
+        for d in range(1, PACK):
+            put(False, 1, d)
+        for d in range(PACK):
+            read_board(d)
+        for d in range(PACK):
+            subtract(d)
+
+        hid = keep.tile([P, O, PACK], BF16, align_bytes=64)
+        across = diff[:].rearrange("p d o -> p o d")
+        half = O // 2
+        nc.scalar.activation(out=hid[:, 0:half, :], in_=across[:, 0:half, :], func=ACT.Abs)
+        nc.vector.scalar_tensor_tensor(
+            out=hid[:, half:O, :], in0=across[:, half:O, :], scalar=-1.0, in1=across[:, half:O, :],
+            op0=ALU.mult, op1=ALU.max,
+        )
+        hid_codes = keep.tile([P, O], U32, align_bytes=64)
+        hid_scales = keep.tile([P, O], U8, align_bytes=64)
+        nc.vector.quantize_mx(
+            out=hid_codes[:].bitcast(FP8X4), scales=hid_scales[:], in_=hid[:].rearrange("p o d -> p (o d)")
+        )
+        for b in range(N // P):
+            nc.tensor.matmul_mx(
+                out=acc[b][:],
+                lhsT=wb_w[:, b * P : (b + 1) * P].bitcast(FP4X4),
+                lhsT_scale=wb_s[:, b * P : (b + 1) * P],
+                rhs=hid_codes[:].bitcast(FP8X4),
+                rhs_scale=hid_scales[:],
+                start=False,
+                stop=True,
+            )
+        res = [keep.tile([P, O], F32, name="res%d" % b) for b in range(N // P)]
+        nc.vector.tensor_copy(out=res[0][:], in_=acc[0][:])
+        nc.sync.dma_start(out=out[0:P, :], in_=res[0][:])
+        nc.scalar.copy(out=res[1][:], in_=acc[1][:])
+        nc.scalar.dma_start(out=out[P : 2 * P, :], in_=res[1][:])

@@ -65,6 +65,11 @@ def tile_picked_respelled_codes_one_boardmixed_reminder_plain_kernel(
         def fetch(dst, window, offsets, factor):
             nc.scalar.activation(out=dst, in_=window[:].indirect(offsets), func=ACT.Copy, scale=factor)
 
+        warm_in = keep.tile([P, 1], F32)
+        warm_out = keep.tile([P, 1], F32)
+        nc.vector.memset(warm_in[:], 0.0)
+        nc.scalar.activation(out=warm_out[:], in_=warm_in[:], func=ACT.Abs)
+
         ua_rows = [load_rows("ua0", ua, 0)]
         l3 = load_list("l3", offs3)
         ha_t = load_factors("ha_t", ha)

@@ -37,9 +37,9 @@ def tile_picked_respelled_codes_one_boardmixed_reminder_plain_kernel(
             nc.sync.dma_start(tile[:], src)
             return tile
 
-        def load_factors(name, src):
+        def load_factors(name, src, queue):
             tile = keep.tile([P, PACK], F32, name=name)
-            nc.sync.dma_start(out=tile[:], in_=src.rearrange("(p t) one -> p (t one)", t=PACK))
+            queue.dma_start(out=tile[:], in_=src.rearrange("(p t) one -> p (t one)", t=PACK))
             return tile
 
         def load_rows(name, src, t):
@@ -48,15 +48,15 @@ def tile_picked_respelled_codes_one_boardmixed_reminder_plain_kernel(
             return tile
 
         def load_words(name, src, dtype, width):
-            tile = keep.tile([P, width], dtype, name=name, align_bytes=64)
+            tile = keep.tile([P, width], dtype, name=name, tag=name, align_bytes=64)
             nc.sync.dma_start(out=tile[:].bitcast(I32), in_=src.bitcast(I32))
             return tile
 
-        def load_scales(name, src):
+        def load_scales(name, src, queue):
             tile = keep.tile([P, src.shape[2]], U8, name=name, align_bytes=64)
             nc.gpsimd.memset(tile[:].bitcast(I32), 0)
             for q in range(4):
-                nc.gpsimd.dma_start(
+                queue.dma_start(
                     out=tile[32 * q : 32 * q + 4, :].bitcast(I32),
                     in_=src[0, 4 * q : 4 * q + 4, :].bitcast(I32),
                 )
@@ -72,26 +72,29 @@ def tile_picked_respelled_codes_one_boardmixed_reminder_plain_kernel(
 
         ua_rows = [load_rows("ua0", ua, 0)]
         l3 = load_list("l3", offs3)
-        ha_t = load_factors("ha_t", ha)
+        ha_t = load_factors("ha_t", ha, nc.sync)
         ua_rows.extend([load_rows("ua%d" % t, ua, t) for t in range(1, PACK)])
         l1 = load_list("l1", offs)
-        ga_t = load_factors("ga_t", ga)
+        ga_t = load_factors("ga_t", ga, nc.sync)
         ta_rows = [load_rows("ta0", ta, 0)]
         l2 = load_list("l2", offs2)
-        gb_t = load_factors("gb_t", gb)
+        gb_rows = gb.rearrange("(p t) one -> p (t one)", t=PACK)
+        gb_t = [keep.tile([P, 2], F32, name="gb_t%d" % u) for u in range(2)]
+        nc.sync.dma_start(out=gb_t[0][:], in_=gb_rows[:, 0:2])
         ta_rows.extend([load_rows("ta%d" % t, ta, t) for t in range(1, PACK)])
+        nc.sync.dma_start(out=gb_t[1][:], in_=gb_rows[:, 2:4])
         xr_w = load_words("xr_w", xr_words[0], U16, Z)
         l7 = load_list("l7", offs7)
         l4 = load_list("l4", offs4)
-        ws_w = load_words("ws_w", ws_words[0].rearrange("p n t -> p (n t)"), U32, N)
-        wb_w = load_words("wb_w", wb_words[0], U16, N)
         l5 = load_list("l5", offs5)
         l6 = load_list("l6", offs6)
-        sa_t = load_factors("sa_t", sa)
-        sb_t = load_factors("sb_t", sb)
-        xr_s = load_scales("xr_s", xr_scales)
-        ws_s = load_scales("ws_s", ws_scales)
-        wb_s = load_scales("wb_s", wb_scales)
+        ws_w = load_words("ws_w", ws_words[0].rearrange("p n t -> p (n t)"), U32, N)
+        wb_w = load_words("wb_w", wb_words[0], U16, N)
+        xr_s = load_scales("xr_s", xr_scales, nc.gpsimd)
+        sa_t = load_factors("sa_t", sa, nc.gpsimd)
+        sb_t = load_factors("sb_t", sb, nc.gpsimd)
+        ws_s = load_scales("ws_s", ws_scales, nc.gpsimd)
+        wb_s = load_scales("wb_s", wb_scales, nc.sync)
 
         board = [keep.tile([P, C], F32, name="board%d" % t) for t in range(PACK)]
         for t in range(PACK):
@@ -114,22 +117,21 @@ def tile_picked_respelled_codes_one_boardmixed_reminder_plain_kernel(
         cols = JH // LIST_ROWS
 
         def fetch_xc(h, t):
-            fetch(xc_rows[h][:, t, :], xcd[t], l2[:, h * cols : (h + 1) * cols], gb_t[:, t : t + 1])
+            fetch(xc_rows[h][:, t, :], xcd[t], l2[:, h * cols : (h + 1) * cols], gb_t[t // 2][:, t % 2 : t % 2 + 1])
 
         for t in range(PACK):
             fetch(xcd[t][:], ta_rows[t], l1[:], ga_t[:, t : t + 1])
             if t > 0:
                 fetch_xc(0, t - 1)
         xc_rows.append(keep.tile([P, PACK, JH], BF16, name="xc_rows1", tag="ta3", align_bytes=64))
-        fetch_xc(1, 0)
         fetch_xc(0, PACK - 1)
-        for t in range(1, PACK):
+        for t in range(PACK):
             fetch_xc(1, t)
 
         xr_gw = keep.tile([P, O], U16, align_bytes=64)
         xr_gs = keep.tile([P, O], U8, align_bytes=64)
-        nc.vector.tensor_copy(out=xr_gw[:], in_=xr_w[:].indirect(l7[:]))
         nc.vector.tensor_copy(out=xr_gs[:], in_=xr_s[:].indirect(l7[:]))
+        nc.vector.tensor_copy(out=xr_gw[:], in_=xr_w[:].indirect(l7[:]))
         acc = [psum.tile([P, O], F32, name="acc%d" % b) for b in range(N // P)]
         for b in range(N // P):
             nc.tensor.matmul_mx(
@@ -145,7 +147,7 @@ def tile_picked_respelled_codes_one_boardmixed_reminder_plain_kernel(
         a_sb = []
         a_ps = []
         for h in range(HALVES):
-            woven = keep.tile([P, JH, PACK], BF16, name="xc_woven%d" % h, tag="xc_woven", align_bytes=64)
+            woven = keep.tile([P, JH, PACK], BF16, name="xc_woven%d" % h, tag="xr_w", align_bytes=64)
             nc.vector.tensor_copy(out=woven[:], in_=xc_rows[h][:].rearrange("p t j -> p j t"))
             codes = keep.tile([P, JH], U32, name="xc_codes%d" % h, align_bytes=64)
             scales = keep.tile([P, JH], U8, name="xc_scales%d" % h, align_bytes=64)
@@ -164,7 +166,7 @@ def tile_picked_respelled_codes_one_boardmixed_reminder_plain_kernel(
                     stop=True,
                 )
             a_ps.append(banks)
-            a_sb.append([keep.tile([P, 2, JH], F32, name="a_sb%d_%d" % (h, u)) for u in range(2)])
+            a_sb.append([keep.tile([P, 2, JH], F32, name="a_sb%d_%d" % (h, u), tag="a_sb%d_%d" % (h, u)) for u in range(2)])
 
         def empty(on_scalar, h, u):
             if on_scalar:
@@ -182,7 +184,7 @@ def tile_picked_respelled_codes_one_boardmixed_reminder_plain_kernel(
 
         first = keep.tile([P, PACK, O], F32)
         second = keep.tile([P, PACK, O], F32)
-        diff = keep.tile([P, PACK, O], F32)
+        diff = keep.tile([P, PACK, O], F32, tag="a_sb1_1")
 
         def read_board(d):
             fetch(first[:, d, :], board[d], l5[:], sa_t[:, d : d + 1])

@@ -72,7 +72,7 @@ def tile_picked_respelled_codes_one_boardmixed_reminder_plain_kernel(
 
         ua_rows = [load_rows("ua0", ua, 0)]
         l3 = load_list("l3", offs3)
-        ha_t = load_factors("ha_t", ha, nc.sync)
+        ha_t = load_factors("ha_t", ha, nc.scalar)
         ua_rows.extend([load_rows("ua%d" % t, ua, t) for t in range(1, PACK)])
         l1 = load_list("l1", offs)
         ga_t = load_factors("ga_t", ga, nc.sync)
@@ -174,9 +174,9 @@ def tile_picked_respelled_codes_one_boardmixed_reminder_plain_kernel(
             else:
                 nc.vector.tensor_copy(out=a_sb[h][u][:], in_=a_ps[h][u][:])
 
-        def put(on_scalar, h, d):
-            dst = board[d][:].indirect(l4[:, h * cols : (h + 1) * cols])
-            src = a_sb[h][d // 2][:, d % 2, :]
+        def put(on_scalar, h, d, lo=0, hi=JH):
+            dst = board[d][:].indirect(l4[:, h * cols + lo // LIST_ROWS : h * cols + hi // LIST_ROWS])
+            src = a_sb[h][d // 2][:, d % 2, lo:hi]
             if on_scalar:
                 nc.scalar.activation(out=dst, in_=src, func=ACT.Copy)
             else:
@@ -197,8 +197,9 @@ def tile_picked_respelled_codes_one_boardmixed_reminder_plain_kernel(
         empty(True, 0, 1)
         put(True, 0, 0)
         put(False, 0, 1)
-        put(True, 0, 3)
+        put(True, 0, 3, 0, JH // 2)
         put(False, 0, 2)
+        put(False, 0, 3, JH // 2, JH)
         empty(True, 1, 0)
         empty(False, 1, 1)
         put(True, 1, 0)

from contextlib import ExitStack

import concourse.mybir as mybir

K, J, R, T, U, F, C, O, N, S, Z = 512, 256, 512, 1024, 512, 1024, 512, 128, 256, 512, 1024
FLOPS = 2 * (K * R * J + R * N * O + S * N * O)

F32 = mybir.dt.float32
BF16 = mybir.dt.bfloat16
I32 = mybir.dt.int32
U32 = mybir.dt.uint32
U16 = mybir.dt.uint16
U8 = mybir.dt.uint8
FP8X4 = mybir.dt.float8_e4m3fn_x4
FP4X4 = mybir.dt.float4_e2m1fn_x4
ACT = mybir.ActivationFunctionType
ALU = mybir.AluOpType

P = 128
PACK = 4
HALVES = 2
JH = J // HALVES
LIST_ROWS = 16


def tile_picked_respelled_codes_one_boardmixed_reminder_plain_kernel(
    tc, ta, ga, gb, ua, ha, sa, sb, wb_words, wb_scales, xr_words, xr_scales, ws_words, ws_scales,
    offs, offs2, offs3, offs4, offs5, offs6, offs7, out,
):
    nc = tc.nc
    with ExitStack() as ctx:
        keep = ctx.enter_context(tc.tile_pool(name="keep", bufs=1))
        psum = ctx.enter_context(tc.psum_pool(name="psum", bufs=1))

        def load_list(name, src):
            tile = keep.tile([P, src.shape[1]], U16, name=name)
            nc.sync.dma_start(tile[:], src)
            return tile

        def load_factors(name, src, queue):
            tile = keep.tile([P, PACK], F32, name=name)
            queue.dma_start(out=tile[:], in_=src.rearrange("(p t) one -> p (t one)", t=PACK))
            return tile

        def load_rows(name, src, t):
            tile = keep.tile([P, src.shape[1]], F32, name=name, tag=name, align_bytes=64)
            nc.sync.dma_start(out=tile[:], in_=src.rearrange("(p t) c -> p t c", t=PACK)[:, t, :])
            return tile

        def load_words(name, src, dtype, width):
            tile = keep.tile([P, width], dtype, name=name, tag=name, align_bytes=64)
            nc.sync.dma_start(out=tile[:].bitcast(I32), in_=src.bitcast(I32))
            return tile

        def load_scales(name, src, queue):
            tile = keep.tile([P, src.shape[2]], U8, name=name, align_bytes=64)
            nc.gpsimd.memset(tile[:].bitcast(I32), 0)
            for q in range(4):
                queue.dma_start(
                    out=tile[32 * q : 32 * q + 4, :].bitcast(I32),
                    in_=src[0, 4 * q : 4 * q + 4, :].bitcast(I32),
                )
            return tile

        def fetch(dst, window, offsets, factor):
            nc.scalar.activation(out=dst, in_=window[:].indirect(offsets), func=ACT.Copy, scale=factor)

        warm_in = keep.tile([P, 1], F32)
        warm_out = keep.tile([P, 1], F32)
        nc.vector.memset(warm_in[:], 0.0)
        nc.scalar.activation(out=warm_out[:], in_=warm_in[:], func=ACT.Abs)

        ua_rows = [load_rows("ua0", ua, 0)]
        l3 = load_list("l3", offs3)
        ha_t = load_factors("ha_t", ha, nc.scalar)
        ua_rows.extend([load_rows("ua%d" % t, ua, t) for t in range(1, PACK)])
        l1 = load_list("l1", offs)
        ga_t = load_factors("ga_t", ga, nc.sync)
        ta_rows = [load_rows("ta0", ta, 0)]
        l2 = load_list("l2", offs2)
        gb_rows = gb.rearrange("(p t) one -> p (t one)", t=PACK)
        gb_t = [keep.tile([P, 2], F32, name="gb_t%d" % u) for u in range(2)]
        nc.sync.dma_start(out=gb_t[0][:], in_=gb_rows[:, 0:2])
        ta_rows.extend([load_rows("ta%d" % t, ta, t) for t in range(1, PACK)])
        nc.sync.dma_start(out=gb_t[1][:], in_=gb_rows[:, 2:4])
        xr_w = load_words("xr_w", xr_words[0], U16, Z)
        l7 = load_list("l7", offs7)
        l4 = load_list("l4", offs4)
        l5 = load_list("l5", offs5)
        l6 = load_list("l6", offs6)
        ws_w = load_words("ws_w", ws_words[0].rearrange("p n t -> p (n t)"), U32, N)
        wb_w = load_words("wb_w", wb_words[0], U16, N)
        xr_s = load_scales("xr_s", xr_scales, nc.gpsimd)
        sa_t = load_factors("sa_t", sa, nc.gpsimd)
        sb_t = load_factors("sb_t", sb, nc.gpsimd)
        ws_s = load_scales("ws_s", ws_scales, nc.gpsimd)
        wb_s = load_scales("wb_s", wb_scales, nc.sync)

        board = [keep.tile([P, C], F32, name="board%d" % t) for t in range(PACK)]
        for t in range(PACK):
            nc.vector.memset(board[t][:], 0.0)

        wc_rows = keep.tile([P, PACK, R], BF16, align_bytes=64)
        for t in range(PACK):
            fetch(wc_rows[:, t, :], ua_rows[t], l3[:], ha_t[:, t : t + 1])
        wc_dealt = keep.tile([P, R * PACK], BF16, align_bytes=64)
        nc.vector.tensor_copy(
            out=wc_dealt[:].rearrange("p (d m t) -> p d m t", d=PACK, t=PACK),
            in_=wc_rows[:].rearrange("p t (m d) -> p d m t", d=PACK),
        )
        wc_codes = keep.tile([P, R], U32, align_bytes=64)
        wc_scales = keep.tile([P, R], U8, align_bytes=64)
        nc.vector.quantize_mx(out=wc_codes[:].bitcast(FP8X4), scales=wc_scales[:], in_=wc_dealt[:])

        xcd = [keep.tile([P, U], F32, name="xcd%d" % t) for t in range(PACK)]
        xc_rows = [keep.tile([P, PACK, JH], BF16, name="xc_rows0", align_bytes=64)]
        cols = JH // LIST_ROWS

        def fetch_xc(h, t):
            fetch(xc_rows[h][:, t, :], xcd[t], l2[:, h * cols : (h + 1) * cols], gb_t[t // 2][:, t % 2 : t % 2 + 1])

        for t in range(PACK):
            fetch(xcd[t][:], ta_rows[t], l1[:], ga_t[:, t : t + 1])
            if t > 0:
                fetch_xc(0, t - 1)
        xc_rows.append(keep.tile([P, PACK, JH], BF16, name="xc_rows1", tag="ta3", align_bytes=64))
        fetch_xc(0, PACK - 1)
        for t in range(PACK):
            fetch_xc(1, t)

        xr_gw = keep.tile([P, O], U16, align_bytes=64)
        xr_gs = keep.tile([P, O], U8, align_bytes=64)
        nc.vector.tensor_copy(out=xr_gs[:], in_=xr_s[:].indirect(l7[:]))
        nc.vector.tensor_copy(out=xr_gw[:], in_=xr_w[:].indirect(l7[:]))
        acc = [psum.tile([P, O], F32, name="acc%d" % b) for b in range(N // P)]
        for b in range(N // P):
            nc.tensor.matmul_mx(
                out=acc[b][:],
                lhsT=ws_w[:, b * P : (b + 1) * P].bitcast(FP8X4),
                lhsT_scale=ws_s[:, b * P : (b + 1) * P],
                rhs=xr_gw[:].bitcast(FP4X4),
                rhs_scale=xr_gs[:],
                start=True,
                stop=False,
            )

        a_sb = []
        a_ps = []
        for h in range(HALVES):
            woven = keep.tile([P, JH, PACK], BF16, name="xc_woven%d" % h, tag="xr_w", align_bytes=64)
            nc.vector.tensor_copy(out=woven[:], in_=xc_rows[h][:].rearrange("p t j -> p j t"))
            codes = keep.tile([P, JH], U32, name="xc_codes%d" % h, align_bytes=64)
            scales = keep.tile([P, JH], U8, name="xc_scales%d" % h, align_bytes=64)
            nc.vector.quantize_mx(
                out=codes[:].bitcast(FP8X4), scales=scales[:], in_=woven[:].rearrange("p j t -> p (j t)")
            )
            banks = [psum.tile([P, 2, JH], F32, name="a_ps%d_%d" % (h, u)) for u in range(2)]
            for d in range(PACK):
                nc.tensor.matmul_mx(
                    out=banks[d // 2][:, d % 2, :],
                    lhsT=wc_codes[:, d * P : (d + 1) * P].bitcast(FP8X4),
                    lhsT_scale=wc_scales[:, d * P : (d + 1) * P],
                    rhs=codes[:].bitcast(FP8X4),
                    rhs_scale=scales[:],
                    start=True,
                    stop=True,
                )
            a_ps.append(banks)
            a_sb.append([keep.tile([P, 2, JH], F32, name="a_sb%d_%d" % (h, u), tag="a_sb%d_%d" % (h, u)) for u in range(2)])

        def empty(on_scalar, h, u):
            if on_scalar:
                nc.scalar.copy(out=a_sb[h][u][:], in_=a_ps[h][u][:])
            else:
                nc.vector.tensor_copy(out=a_sb[h][u][:], in_=a_ps[h][u][:])

        def put(on_scalar, h, d, lo=0, hi=JH):
            dst = board[d][:].indirect(l4[:, h * cols + lo // LIST_ROWS : h * cols + hi // LIST_ROWS])
            src = a_sb[h][d // 2][:, d % 2, lo:hi]
            if on_scalar:
                nc.scalar.activation(out=dst, in_=src, func=ACT.Copy)
            else:
                nc.vector.tensor_copy(out=dst, in_=src)

        first = keep.tile([P, PACK, O], F32)
        second = keep.tile([P, PACK, O], F32)
        diff = keep.tile([P, PACK, O], F32, tag="a_sb1_1")

        def read_board(d):
            fetch(first[:, d, :], board[d], l5[:], sa_t[:, d : d + 1])
            fetch(second[:, d, :], board[d], l6[:], sb_t[:, d : d + 1])

        def subtract(d):
            nc.vector.tensor_tensor(out=diff[:, d, :], in0=first[:, d, :], in1=second[:, d, :], op=ALU.subtract)

        empty(True, 0, 0)
        empty(True, 0, 1)
        put(True, 0, 0)
        put(False, 0, 1)
        put(True, 0, 3, 0, JH // 2)
        put(False, 0, 2)
        put(False, 0, 3, JH // 2, JH)
        empty(True, 1, 0)
        empty(False, 1, 1)
        put(True, 1, 0)
        for d in range(1, PACK):
            put(False, 1, d)
        for d in range(PACK):
            read_board(d)
        for d in range(PACK):
            subtract(d)

        hid = keep.tile([P, O, PACK], BF16, align_bytes=64)
        across = diff[:].rearrange("p d o -> p o d")
        half = O // 2
        nc.scalar.activation(out=hid[:, 0:half, :], in_=across[:, 0:half, :], func=ACT.Abs)
        nc.vector.scalar_tensor_tensor(
            out=hid[:, half:O, :], in0=across[:, half:O, :], scalar=-1.0, in1=across[:, half:O, :],
            op0=ALU.mult, op1=ALU.max,
        )
        hid_codes = keep.tile([P, O], U32, align_bytes=64)
        hid_scales = keep.tile([P, O], U8, align_bytes=64)
        nc.vector.quantize_mx(
            out=hid_codes[:].bitcast(FP8X4), scales=hid_scales[:], in_=hid[:].rearrange("p o d -> p (o d)")
        )
        for b in range(N // P):
            nc.tensor.matmul_mx(
                out=acc[b][:],
                lhsT=wb_w[:, b * P : (b + 1) * P].bitcast(FP4X4),
                lhsT_scale=wb_s[:, b * P : (b + 1) * P],
                rhs=hid_codes[:].bitcast(FP8X4),
                rhs_scale=hid_scales[:],
                start=False,
                stop=True,
            )
        res = [keep.tile([P, O], F32, name="res%d" % b) for b in range(N // P)]
        nc.vector.tensor_copy(out=res[0][:], in_=acc[0][:])
        nc.sync.dma_start(out=out[0:P, :], in_=res[0][:])
        nc.scalar.copy(out=res[1][:], in_=acc[1][:])
        nc.scalar.dma_start(out=out[P : 2 * P, :], in_=res[1][:])
